import numpy as np
import ml_dtypes


def mxq(x, axis, fmt="e4m3"):
    dtype, down = {"e4m3": (ml_dtypes.float8_e4m3fn, 7), "e5m2": (ml_dtypes.float8_e5m2, 14)}[fmt]
    v = np.moveaxis(np.asarray(x, np.float32).astype(ml_dtypes.bfloat16).astype(np.float64), axis, -1)
    blocks = v.reshape(v.shape[:-1] + (-1, 32))
    amax = np.abs(blocks).max(-1, keepdims=True)
    byte = np.maximum(np.where(amax > 0, np.frexp(amax)[1] - 1 + 127, 0) - down, 1)
    scale = np.exp2(byte - 127.0)
    codes = (blocks / scale).astype(np.float32).astype(dtype).astype(np.float64)
    return np.moveaxis((codes * scale).reshape(v.shape), -1, axis)


WIDE = False


def mx_kscale(k):
    if not WIDE:
        return np.ones(k)
    levels = np.array([10, -10, 5, -5, 0])
    if k % 512:
        return np.exp2(np.random.permutation(np.resize(levels, k // 32))).repeat(32)
    a = np.empty((k // 512, 16))
    for p in range(k // 512):
        a[p, :8] = np.random.permutation(np.resize(levels, 8))
        for g in range(8):
            far = levels[np.abs(levels - a[p, g]) >= 10]
            a[p, g + 8] = far[np.random.randint(len(far))]
    return np.exp2(a.ravel()).repeat(32)


def f64(x):
    return np.asarray(x).astype(np.float64)


def striped(idx):
    return np.tile(idx.reshape(-1, 16).T, (8, 1)).astype(np.uint16)


def unstriped(offs):
    return offs[:16].T.reshape(-1).astype(np.int64)


def pack_weight(w):
    k, n = w.shape
    w = f64(np.asarray(w, np.float32).astype(ml_dtypes.bfloat16)).reshape(k // 32, 32, n)
    amax = np.abs(w).max(1)
    byte = np.clip(np.where(amax > 0, np.frexp(amax)[1] - 1 + 127 - 7, 1), 1, 254)
    scaled = (w * np.exp2(127.0 - byte)[:, None, :]).reshape(k, n).astype(np.float32)
    words = np.ascontiguousarray(scaled.reshape(k // 512, 128, 4, n).transpose(0, 1, 3, 2)).astype(ml_dtypes.float8_e4m3fn).view(np.uint8)
    return words, np.ascontiguousarray(byte.astype(np.uint8).reshape(k // 512, 16, n))


def unpack_weight(words, scales):
    g, p, n, _ = words.shape
    vals = np.ascontiguousarray(words).view(ml_dtypes.float8_e4m3fn).astype(np.float64) * np.repeat(np.exp2(scales.astype(np.float64) - 127.0), 8, axis=1)[..., None]
    return vals.transpose(0, 1, 3, 2).reshape(g * 512, n)


K, T, S, N, H, U = 512, 1024, 512, 256, 512, 1024


def setup_inputs():
    n = np.random.standard_normal
    s = mx_kscale(K)[:, None]
    u = mx_kscale(H)
    packed_xT = pack_weight(n((K, T)) * s)
    return {
        "x_words": packed_xT[0],
        "x_scales": packed_xT[1],
        "w1": (n((K, H)) / np.sqrt(K) / s).astype(np.float32),
        "w2": (n((K, H)) / np.sqrt(K) / s).astype(np.float32),
        "sin2": (np.random.uniform(0.0, 0.6, (H, U))).astype(np.float32),
        "unit": (np.random.uniform(0.6, 1.4, (H, 1)) * u[:, None]).astype(np.float32),
        "w3": (n((H, N)) / np.sqrt(H) / u[:, None]).astype(np.float32),
        "offs": striped(np.random.permutation(T)[:S]),
        "up": striped(np.random.permutation(np.concatenate([np.arange(S), np.random.randint(0, S, U - S)]))),
        "dn": striped(np.random.permutation(np.concatenate([np.arange(S), np.random.randint(0, S, U - S)]))),
    }


def reference(x_words, x_scales, w1, w2, sin2, unit, w3, offs, up, dn):
    xq = unpack_weight(x_words, x_scales)[:, unstriped(offs)]
    vp = mxq(f64(w1), 0, "e4m3").T @ xq
    velp = np.exp(0.5 * np.tanh(vp))
    pd = velp[:, unstriped(dn)]
    pu = velp[:, unstriped(up)]
    r0 = (pd - pu) / (pd + pu)
    vs = mxq(f64(w2), 0, "e4m3").T @ xq
    vels = np.exp(0.5 * np.tanh(vs))
    sd = vels[:, unstriped(dn)]
    su = vels[:, unstriped(up)]
    pm = pu + pd
    grad = r0 - (2.0 * (((sd) ** 2 - ((su) ** 2)) / ((pm) ** 2)))
    amp = r0 + grad * f64(sin2)
    hid = f64(unit) * amp
    return mxq(f64(w3), 0, "e4m3").T @ mxq(hid, 0, "e4m3")

@@ -1,0 +1,222 @@
+from contextlib import ExitStack
+
+import concourse.mybir as mybir
+
+K, T, S, N, H, U = 512, 1024, 512, 256, 512, 1024
+FLOPS = 2 * K * H * S * 2 + 2 * H * N * U
+
+F32 = mybir.dt.float32
+BF16 = mybir.dt.bfloat16
+I32 = mybir.dt.int32
+U32 = mybir.dt.uint32
+U16 = mybir.dt.uint16
+U8 = mybir.dt.uint8
+FP8X4 = mybir.dt.float8_e4m3fn_x4
+ACT = mybir.ActivationFunctionType
+ALU = mybir.AluOpType
+
+P = 128
+PACK = 4
+SPARE = 16
+CHUNKS = (512, 256, 256)
+
+
+def tile_picked_yshuey_amp_p_kernel(
+    tc, x_words, x_scales, w1, w2, sin2, unit, w3, offs, up, dn, out
+):
+    nc = tc.nc
+    with ExitStack() as ctx:
+        keep = ctx.enter_context(tc.tile_pool(name="keep", bufs=1))
+        work = ctx.enter_context(tc.tile_pool(name="work", bufs=4))
+        stage = ctx.enter_context(tc.tile_pool(name="stage", bufs=2))
+        psum = ctx.enter_context(tc.psum_pool(name="psum", bufs=4))
+
+        offs_t = keep.tile([P, S // 16], U16, name="offs_t")
+        up_t = keep.tile([P, U // 16], U16, name="up_t")
+        dn_t = keep.tile([P, U // 16], U16, name="dn_t")
+        xw = keep.tile([P, T], U32, name="xw")
+        xs = keep.tile([P, T], U8, name="xs")
+        unit_t = keep.tile([P, PACK], F32, name="unit_t")
+        half = H // 2
+        w1_raw = [keep.tile([P, PACK, half], F32, name=f"w1_raw{a}") for a in range(2)]
+        w2_raw = [keep.tile([P, PACK, half], F32, name=f"w2_raw{a}") for a in range(2)]
+        w3_raw = keep.tile([P, PACK, N], F32, name="w3_raw")
+        starts = [sum(CHUNKS[:c]) for c in range(len(CHUNKS))]
+        sin_t = [keep.tile([P, PACK, n], F32, name=f"sin{c}") for c, n in enumerate(CHUNKS)]
+        tan_p = [keep.tile([P, S + SPARE], F32, name=f"tan_p{j}") for j in range(PACK)]
+        sq_s = [keep.tile([P, S + SPARE], F32, name=f"sq_s{j}") for j in range(PACK)]
+
+        nc.vector.memset(xs[:].bitcast(I32), 0)
+        for win in tan_p + sq_s:
+            nc.gpsimd.memset(win[:, S:], 0.0)
+
+        nc.sync.dma_start(offs_t[:], offs)
+        nc.sync.dma_start(xw[:].bitcast(I32), x_words[0].rearrange("p n t -> p (n t)").bitcast(I32))
+        for q in range(4):
+            nc.sync.dma_start(xs[32 * q : 32 * q + 4, :].bitcast(I32), x_scales[0, 4 * q : 4 * q + 4, :].bitcast(I32))
+        w1_v = w1.rearrange("(p j) c -> p j c", j=PACK)
+        w2_v = w2.rearrange("(p j) c -> p j c", j=PACK)
+        sin_v = sin2.rearrange("(p j) r -> p j r", j=PACK)
+        for a in range(2):
+            nc.sync.dma_start(w1_raw[a][:], w1_v[:, :, a * half : (a + 1) * half])
+        nc.sync.dma_start(up_t[:], up)
+        nc.sync.dma_start(dn_t[:], dn)
+        for a in range(2):
+            nc.sync.dma_start(w2_raw[a][:], w2_v[:, :, a * half : (a + 1) * half])
+        nc.sync.dma_start(unit_t[:], unit.rearrange("(p j) o -> p (j o)", j=PACK))
+        nc.sync.dma_start(sin_t[0][:], sin_v[:, :, 0 : CHUNKS[0]])
+        nc.sync.dma_start(w3_raw[:], w3.rearrange("(p j) c -> p j c", j=PACK))
+        for c in range(1, len(CHUNKS)):
+            nc.sync.dma_start(sin_t[c][:], sin_v[:, :, starts[c] : starts[c] + CHUNKS[c]])
+
+        xg = keep.tile([P, S], U32, name="xg", align_bytes=64)
+        xsg = keep.tile([P, S], U8, name="xsg", align_bytes=64)
+        nc.vector.tensor_copy(xg[:], xw[:].indirect(offs_t[:]))
+        nc.vector.tensor_copy(xsg[:], xs[:].indirect(offs_t[:]))
+
+        def dealt_weights(raw, name, copies):
+            grouped = keep.tile([P, PACK * H], BF16, name=name + "_g", align_bytes=64)
+            codes = keep.tile([P, H], U32, name=name + "_c", align_bytes=64)
+            scales = keep.tile([P, H], U8, name=name + "_s", align_bytes=64)
+            view = grouped[:].rearrange("p (t m j) -> p m t j", t=PACK, j=PACK)
+            for a in range(2):
+                copies[a](view[:, a * 64 : (a + 1) * 64], raw[a][:].rearrange("p j (m t) -> p m t j", t=PACK))
+            for lo, hi in ((0, P), (P, H)):
+                nc.vector.quantize_mx(codes[:, lo:hi].bitcast(FP8X4), scales[:, lo:hi], grouped[:, PACK * lo : PACK * hi])
+            return codes, scales
+
+        def product(weights, j):
+            codes, scales = weights
+            acc = psum.tile([P, S], F32, name="acc")
+            nc.tensor.matmul_mx(
+                acc[:], lhsT=codes[:, j * P : (j + 1) * P].bitcast(FP8X4), lhsT_scale=scales[:, j * P : (j + 1) * P],
+                rhs=xg[:].bitcast(FP8X4), rhs_scale=xsg[:], start=True, stop=True,
+            )
+            return acc
+
+        q1 = dealt_weights(w1_raw, "w1", (nc.vector.tensor_copy, nc.scalar.copy))
+        q2 = dealt_weights(w2_raw, "w2", (nc.vector.tensor_copy, nc.vector.tensor_copy))
+        neg_half_unit = keep.tile([P, PACK], F32, name="neg_half_unit")
+        nc.vector.tensor_scalar(neg_half_unit[:], unit_t[:], -0.5, None, ALU.mult)
+
+        units = [(c, j) for c in range(len(CHUNKS)) for j in range(PACK)]
+        st = [{} for u in units]
+        hid = {}
+
+        def tile_of(n, key):
+            st[n][key] = work.tile([P, CHUNKS[units[n][0]]], F32, name=key)
+            return st[n][key][:]
+
+        def cols(lst, n):
+            c = units[n][0]
+            return lst[:, starts[c] // 16 : (starts[c] + CHUNKS[c]) // 16]
+
+        def p_window(j):
+            nc.scalar.activation(tan_p[j][:, :S], product(q1, j)[:], ACT.Tanh)
+
+        def s_window(j):
+            tan_s = stage.tile([P, S], F32, name="tan_s")
+            nc.scalar.activation(tan_s[:], product(q2, j)[:], ACT.Tanh)
+            nc.scalar.activation(sq_s[j][:, :S], tan_s[:], ACT.Exp)
+
+        def a1(n):
+            nc.scalar.activation(tile_of(n, "ntu"), tan_p[units[n][1]][:].indirect(cols(up_t, n)), ACT.Copy, scale=-1.0)
+
+        def a2(n):
+            nc.scalar.activation(tile_of(n, "nqu"), sq_s[units[n][1]][:].indirect(cols(up_t, n)), ACT.Copy, scale=-1.0)
+
+        def a3(n):
+            nc.scalar.activation(tile_of(n, "e"), st[n]["ntu"][:], ACT.Exp)
+
+        def a4(n):
+            nc.scalar.activation(tile_of(n, "r0"), st[n]["dt"][:], ACT.Tanh, scale=0.25)
+
+        def a5(n):
+            nc.scalar.activation(tile_of(n, "c4"), st[n]["r0"][:], ACT.Square, bias=-1.0)
+
+        def b1(n):
+            nc.vector.tensor_tensor(tile_of(n, "dt"), tan_p[units[n][1]][:].indirect(cols(dn_t, n)), st[n]["ntu"][:], ALU.add)
+
+        def b2(n):
+            nc.vector.tensor_tensor(tile_of(n, "dq"), sq_s[units[n][1]][:].indirect(cols(dn_t, n)), st[n]["nqu"][:], ALU.add)
+
+        def b3(n):
+            nc.vector.tensor_tensor(tile_of(n, "de"), st[n]["dq"][:], st[n]["e"][:], ALU.mult)
+
+        def b4(n):
+            j = units[n][1]
+            nc.vector.scalar_tensor_tensor(tile_of(n, "y"), st[n]["de"][:], neg_half_unit[:, j : j + 1], st[n]["c4"][:], ALU.mult, ALU.mult)
+
+        def b5(n):
+            j = units[n][1]
+            nc.vector.scalar_tensor_tensor(tile_of(n, "g"), st[n]["r0"][:], unit_t[:, j : j + 1], st[n]["y"][:], ALU.mult, ALU.add)
+
+        def b6(n):
+            c, j = units[n]
+            nc.vector.tensor_tensor(tile_of(n, "gs"), st[n]["g"][:], sin_t[c][:, j, :], ALU.mult)
+
+        def b7(n):
+            c, j = units[n]
+            if j == 0:
+                hid[c] = stage.tile([P, PACK, CHUNKS[c]], BF16, name="hid")
+            nc.vector.scalar_tensor_tensor(hid[c][:, j, :], st[n]["r0"][:], unit_t[:, j : j + 1], st[n]["gs"][:], ALU.mult, ALU.add)
+
+        w3_q = []
+
+        def prepare_w3():
+            grouped = keep.tile([P, N, PACK], BF16, name="w3_g", align_bytes=64)
+            codes = keep.tile([P, N], U32, name="w3_c", align_bytes=64)
+            scales = keep.tile([P, N], U8, name="w3_s", align_bytes=64)
+            nc.vector.tensor_copy(
+                grouped[:].rearrange("p (c i) t -> p c t i", i=4), w3_raw[:].rearrange("p t (c i) -> p c t i", i=4)
+            )
+            nc.vector.quantize_mx(codes[:].bitcast(FP8X4), scales[:], grouped[:].rearrange("p n t -> p (n t)"))
+            w3_q.extend([codes, scales])
+
+        def finish(c):
+            n = CHUNKS[c]
+            woven = stage.tile([P, n, PACK], BF16, name="woven", align_bytes=64)
+            codes = stage.tile([P, n], U32, name="hid_c", align_bytes=64)
+            scales = stage.tile([P, n], U8, name="hid_s", align_bytes=64)
+            (nc.scalar.copy if c == 0 else nc.vector.tensor_copy)(
+                woven[:].rearrange("p (c i) t -> p c t i", i=4), hid[c][:].rearrange("p t (c i) -> p c t i", i=4)
+            )
+            nc.vector.quantize_mx(codes[:].bitcast(FP8X4), scales[:], woven[:].rearrange("p n t -> p (n t)"))
+            for a in range(N // P):
+                acc = psum.tile([P, n], F32, name="acc_out")
+                nc.tensor.matmul_mx(
+                    acc[:], lhsT=w3_q[0][:, a * P : (a + 1) * P].bitcast(FP8X4), lhsT_scale=w3_q[1][:, a * P : (a + 1) * P],
+                    rhs=codes[:].bitcast(FP8X4), rhs_scale=scales[:], start=True, stop=True,
+                )
+                res = work.tile([P, n], F32, name="res")
+                nc.scalar.copy(res[:], acc[:])
+                nc.sync.dma_start(out[a * P : (a + 1) * P, starts[c] : starts[c] + n], res[:])
+
+        def step(fn, n):
+            if 0 <= n < len(units):
+                fn(n)
+
+        p_window(0)
+        a1(0)
+        p_window(1)
+        for n in range(-2, len(units) + 1):
+            if 0 <= n + 2 < PACK:
+                s_window(n + 2)
+            if 2 <= n + 4 < PACK:
+                p_window(n + 4)
+            step(a1, n + 3)
+            step(b3, n)
+            step(b5, n - 1)
+            step(b1, n + 2)
+            step(a4, n + 2)
+            step(a2, n + 2)
+            step(b4, n)
+            step(b6, n - 1)
+            step(a3, n + 2)
+            step(b2, n + 1)
+            step(a5, n + 2)
+            step(b7, n - 1)
+            if n == 1:
+                prepare_w3()
+            if n >= 1 and units[n - 1][1] == PACK - 1:
+                finish(units[n - 1][0])

@@ -17,8 +17,14 @@ ALU = mybir.AluOpType
 
 P = 128
 PACK = 4
-SPARE = 16
+GROUP = 16
+WINDOW = S + GROUP
+
 CHUNKS = (512, 256, 256)
+PIECES = ((0, 256), (0, 256), (0, 512), (1, 512), (1, 512)) + tuple((j, n) for n in CHUNKS for j in (2, 3))
+HEAD, TAIL = 2, 4
+FETCH_BUFS = 3
+WORK_BUFS = 5
 
 
 def tile_picked_yshuey_amp_p_kernel(
@@ -27,13 +33,13 @@ def tile_picked_yshuey_amp_p_kernel(
     nc = tc.nc
     with ExitStack() as ctx:
         keep = ctx.enter_context(tc.tile_pool(name="keep", bufs=1))
-        work = ctx.enter_context(tc.tile_pool(name="work", bufs=4))
-        stage = ctx.enter_context(tc.tile_pool(name="stage", bufs=2))
+        work = ctx.enter_context(tc.tile_pool(name="work", bufs=WORK_BUFS))
+        stage = ctx.enter_context(tc.tile_pool(name="stage", bufs=len(CHUNKS)))
         psum = ctx.enter_context(tc.psum_pool(name="psum", bufs=4))
 
-        offs_t = keep.tile([P, S // 16], U16, name="offs_t")
-        up_t = keep.tile([P, U // 16], U16, name="up_t")
-        dn_t = keep.tile([P, U // 16], U16, name="dn_t")
+        offs_t = keep.tile([P, S // GROUP], U16, name="offs_t")
+        up_t = keep.tile([P, U // GROUP], U16, name="up_t")
+        dn_t = keep.tile([P, U // GROUP], U16, name="dn_t")
         xw = keep.tile([P, T], U32, name="xw")
         xs = keep.tile([P, T], U8, name="xs")
         unit_t = keep.tile([P, PACK], F32, name="unit_t")
@@ -42,13 +48,13 @@ def tile_picked_yshuey_amp_p_kernel(
         w2_raw = [keep.tile([P, PACK, half], F32, name=f"w2_raw{a}") for a in range(2)]
         w3_raw = keep.tile([P, PACK, N], F32, name="w3_raw")
         starts = [sum(CHUNKS[:c]) for c in range(len(CHUNKS))]
-        sin_t = [keep.tile([P, PACK, n], F32, name=f"sin{c}") for c, n in enumerate(CHUNKS)]
-        tan_p = [keep.tile([P, S + SPARE], F32, name=f"tan_p{j}") for j in range(PACK)]
-        sq_s = [keep.tile([P, S + SPARE], F32, name=f"sq_s{j}") for j in range(PACK)]
+        sin_t = [keep.tile([P, U], F32, name=f"sin{j}") for j in range(PACK)]
+        tp_table = [keep.tile([P, WINDOW], F32, name=f"tp_table{j}") for j in range(PACK)]
+        sq_table = [keep.tile([P, WINDOW], F32, name=f"sq_table{j}") for j in range(PACK)]
 
         nc.vector.memset(xs[:].bitcast(I32), 0)
-        for win in tan_p + sq_s:
-            nc.gpsimd.memset(win[:, S:], 0.0)
+        for table in tp_table + sq_table:
+            nc.gpsimd.memset(table[:, S:], 0.0)
 
         nc.sync.dma_start(offs_t[:], offs)
         nc.sync.dma_start(xw[:].bitcast(I32), x_words[0].rearrange("p n t -> p (n t)").bitcast(I32))
@@ -64,10 +70,9 @@ def tile_picked_yshuey_amp_p_kernel(
         for a in range(2):
             nc.sync.dma_start(w2_raw[a][:], w2_v[:, :, a * half : (a + 1) * half])
         nc.sync.dma_start(unit_t[:], unit.rearrange("(p j) o -> p (j o)", j=PACK))
-        nc.sync.dma_start(sin_t[0][:], sin_v[:, :, 0 : CHUNKS[0]])
         nc.sync.dma_start(w3_raw[:], w3.rearrange("(p j) c -> p j c", j=PACK))
-        for c in range(1, len(CHUNKS)):
-            nc.sync.dma_start(sin_t[c][:], sin_v[:, :, starts[c] : starts[c] + CHUNKS[c]])
+        for j in range(PACK):
+            nc.sync.dma_start(sin_t[j][:], sin_v[:, j, :])
 
         xg = keep.tile([P, S], U32, name="xg", align_bytes=64)
         xsg = keep.tile([P, S], U8, name="xsg", align_bytes=64)
@@ -79,8 +84,9 @@ def tile_picked_yshuey_amp_p_kernel(
             codes = keep.tile([P, H], U32, name=name + "_c", align_bytes=64)
             scales = keep.tile([P, H], U8, name=name + "_s", align_bytes=64)
             view = grouped[:].rearrange("p (t m j) -> p m t j", t=PACK, j=PACK)
+            m_half = half // PACK
             for a in range(2):
-                copies[a](view[:, a * 64 : (a + 1) * 64], raw[a][:].rearrange("p j (m t) -> p m t j", t=PACK))
+                copies[a](view[:, a * m_half : (a + 1) * m_half], raw[a][:].rearrange("p j (m t) -> p m t j", t=PACK))
             for lo, hi in ((0, P), (P, H)):
                 nc.vector.quantize_mx(codes[:, lo:hi].bitcast(FP8X4), scales[:, lo:hi], grouped[:, PACK * lo : PACK * hi])
             return codes, scales
@@ -94,129 +100,126 @@ def tile_picked_yshuey_amp_p_kernel(
             )
             return acc
 
-        q1 = dealt_weights(w1_raw, "w1", (nc.vector.tensor_copy, nc.scalar.copy))
-        q2 = dealt_weights(w2_raw, "w2", (nc.vector.tensor_copy, nc.vector.tensor_copy))
+        w1_q = dealt_weights(w1_raw, "w1", (nc.scalar.copy, nc.vector.tensor_copy))
+        w2_q = dealt_weights(w2_raw, "w2", (nc.vector.tensor_copy, nc.vector.tensor_copy))
         neg_half_unit = keep.tile([P, PACK], F32, name="neg_half_unit")
         nc.vector.tensor_scalar(neg_half_unit[:], unit_t[:], -0.5, None, ALU.mult)
 
-        units = [(c, j) for c in range(len(CHUNKS)) for j in range(PACK)]
-        st = [{} for u in units]
-        hid = {}
+        pieces = [(j, sum(w for i, w in PIECES[:k] if i == j), width) for k, (j, width) in enumerate(PIECES)]
+        held = [{} for piece in pieces]
+        hid = [keep.tile([P, PACK, size], BF16, name=f"hid{c}") for c, size in enumerate(CHUNKS)]
 
-        def tile_of(n, key):
-            st[n][key] = work.tile([P, CHUNKS[units[n][0]]], F32, name=key)
-            return st[n][key][:]
+        def new(n, key, bufs=WORK_BUFS):
+            held[n][key] = work.tile([P, pieces[n][2]], F32, name=key, bufs=bufs)
+            return held[n][key][:]
 
-        def cols(lst, n):
-            c = units[n][0]
-            return lst[:, starts[c] // 16 : (starts[c] + CHUNKS[c]) // 16]
+        def looked_up(tables, lst, n):
+            j, lo, width = pieces[n]
+            return tables[j][:].indirect(lst[:, lo // GROUP : (lo + width) // GROUP])
 
-        def p_window(j):
-            nc.scalar.activation(tan_p[j][:, :S], product(q1, j)[:], ACT.Tanh)
+        def fetch_up(tables, n, key):
+            if n < HEAD:
+                nc.vector.tensor_copy(new(n, key, FETCH_BUFS), looked_up(tables, up_t, n))
+            else:
+                nc.scalar.activation(new(n, key, FETCH_BUFS), looked_up(tables, up_t, n), ACT.Copy, scale=-1.0)
 
-        def s_window(j):
-            tan_s = stage.tile([P, S], F32, name="tan_s")
-            nc.scalar.activation(tan_s[:], product(q2, j)[:], ACT.Tanh)
-            nc.scalar.activation(sq_s[j][:, :S], tan_s[:], ACT.Exp)
+        def minus_up(n):
+            return ALU.subtract if n < HEAD else ALU.add
 
-        def a1(n):
-            nc.scalar.activation(tile_of(n, "ntu"), tan_p[units[n][1]][:].indirect(cols(up_t, n)), ACT.Copy, scale=-1.0)
+        def fetch_tp_up(n):
+            j, lo, width = pieces[n]
+            if lo == 0:
+                nc.scalar.activation(tp_table[j][:, :S], product(w1_q, j)[:], ACT.Tanh)
+            fetch_up(tp_table, n, "tp_up")
 
-        def a2(n):
-            nc.scalar.activation(tile_of(n, "nqu"), sq_s[units[n][1]][:].indirect(cols(up_t, n)), ACT.Copy, scale=-1.0)
+        def fetch_sq_up(n):
+            j, lo, width = pieces[n]
+            if lo == 0:
+                tan_s = stage.tile([P, S], F32, name="tan_s")
+                nc.scalar.activation(tan_s[:], product(w2_q, j)[:], ACT.Tanh)
+                nc.scalar.activation(sq_table[j][:, :S], tan_s[:], ACT.Exp)
+            fetch_up(sq_table, n, "sq_up")
+            if n >= len(pieces) - TAIL:
+                nc.scalar.activation(new(n, "sq_dn", FETCH_BUFS), looked_up(sq_table, dn_t, n), ACT.Copy)
 
-        def a3(n):
-            nc.scalar.activation(tile_of(n, "e"), st[n]["ntu"][:], ACT.Exp)
+        def inverse_square(n):
+            nc.scalar.activation(new(n, "inv_pu2"), held[n]["tp_up"][:], ACT.Exp, scale=-1.0 if n < HEAD else 1.0)
 
-        def a4(n):
-            nc.scalar.activation(tile_of(n, "r0"), st[n]["dt"][:], ACT.Tanh, scale=0.25)
+        def normal_reflection(n):
+            nc.scalar.activation(new(n, "r0"), held[n]["tp_diff"][:], ACT.Tanh, scale=0.25)
 
-        def a5(n):
-            nc.scalar.activation(tile_of(n, "c4"), st[n]["r0"][:], ACT.Square, bias=-1.0)
+        def share_square(n):
+            nc.scalar.activation(new(n, "share2"), held[n]["r0"][:], ACT.Square, bias=-1.0)
 
-        def b1(n):
-            nc.vector.tensor_tensor(tile_of(n, "dt"), tan_p[units[n][1]][:].indirect(cols(dn_t, n)), st[n]["ntu"][:], ALU.add)
+        def tp_difference(n):
+            nc.vector.tensor_tensor(new(n, "tp_diff"), looked_up(tp_table, dn_t, n), held[n]["tp_up"][:], minus_up(n))
 
-        def b2(n):
-            nc.vector.tensor_tensor(tile_of(n, "dq"), sq_s[units[n][1]][:].indirect(cols(dn_t, n)), st[n]["nqu"][:], ALU.add)
+        def sq_difference(n):
+            lower = held[n]["sq_dn"][:] if "sq_dn" in held[n] else looked_up(sq_table, dn_t, n)
+            nc.vector.tensor_tensor(new(n, "chain"), lower, held[n]["sq_up"][:], minus_up(n))
 
-        def b3(n):
-            nc.vector.tensor_tensor(tile_of(n, "de"), st[n]["dq"][:], st[n]["e"][:], ALU.mult)
+        def over_pu2(n):
+            chain = held[n]["chain"][:]
+            nc.vector.tensor_tensor(chain, chain, held[n]["inv_pu2"][:], ALU.mult)
 
-        def b4(n):
-            j = units[n][1]
-            nc.vector.scalar_tensor_tensor(tile_of(n, "y"), st[n]["de"][:], neg_half_unit[:, j : j + 1], st[n]["c4"][:], ALU.mult, ALU.mult)
+        def shear_term(n):
+            j, chain = pieces[n][0], held[n]["chain"][:]
+            nc.vector.scalar_tensor_tensor(chain, chain, neg_half_unit[:, j : j + 1], held[n]["share2"][:], ALU.mult, ALU.mult)
 
-        def b5(n):
-            j = units[n][1]
-            nc.vector.scalar_tensor_tensor(tile_of(n, "g"), st[n]["r0"][:], unit_t[:, j : j + 1], st[n]["y"][:], ALU.mult, ALU.add)
+        def gradient(n):
+            j, chain = pieces[n][0], held[n]["chain"][:]
+            nc.vector.scalar_tensor_tensor(chain, held[n]["r0"][:], unit_t[:, j : j + 1], chain, ALU.mult, ALU.add)
 
-        def b6(n):
-            c, j = units[n]
-            nc.vector.tensor_tensor(tile_of(n, "gs"), st[n]["g"][:], sin_t[c][:, j, :], ALU.mult)
+        def times_sin2(n):
+            j, lo, width = pieces[n]
+            chain = held[n]["chain"][:]
+            nc.vector.tensor_tensor(chain, chain, sin_t[j][:, lo : lo + width], ALU.mult)
 
-        def b7(n):
-            c, j = units[n]
-            if j == 0:
-                hid[c] = stage.tile([P, PACK, CHUNKS[c]], BF16, name="hid")
-            nc.vector.scalar_tensor_tensor(hid[c][:, j, :], st[n]["r0"][:], unit_t[:, j : j + 1], st[n]["gs"][:], ALU.mult, ALU.add)
+        def hidden(n):
+            j, lo, width = pieces[n]
+            for c, size in enumerate(CHUNKS):
+                first, last = max(lo, starts[c]), min(lo + width, starts[c] + size)
+                if first < last:
+                    nc.vector.scalar_tensor_tensor(
+                        hid[c][:, j, first - starts[c] : last - starts[c]], held[n]["r0"][:, first - lo : last - lo],
+                        unit_t[:, j : j + 1], held[n]["chain"][:, first - lo : last - lo], ALU.mult, ALU.add,
+                    )
 
-        w3_q = []
+        def weave(copy, woven, rows):
+            copy(woven[:].rearrange("p (c i) j -> p c j i", i=4), rows[:].rearrange("p j (c i) -> p c j i", i=4))
 
-        def prepare_w3():
-            grouped = keep.tile([P, N, PACK], BF16, name="w3_g", align_bytes=64)
-            codes = keep.tile([P, N], U32, name="w3_c", align_bytes=64)
-            scales = keep.tile([P, N], U8, name="w3_s", align_bytes=64)
-            nc.vector.tensor_copy(
-                grouped[:].rearrange("p (c i) t -> p c t i", i=4), w3_raw[:].rearrange("p t (c i) -> p c t i", i=4)
-            )
-            nc.vector.quantize_mx(codes[:].bitcast(FP8X4), scales[:], grouped[:].rearrange("p n t -> p (n t)"))
-            w3_q.extend([codes, scales])
+        w3_woven = keep.tile([P, N, PACK], BF16, name="w3_g", align_bytes=64)
+        w3_codes = keep.tile([P, N], U32, name="w3_c", align_bytes=64)
+        w3_scales = keep.tile([P, N], U8, name="w3_s", align_bytes=64)
+        weave(nc.vector.tensor_copy, w3_woven, w3_raw)
+        nc.vector.quantize_mx(w3_codes[:].bitcast(FP8X4), w3_scales[:], w3_woven[:].rearrange("p n t -> p (n t)"))
 
         def finish(c):
-            n = CHUNKS[c]
-            woven = stage.tile([P, n, PACK], BF16, name="woven", align_bytes=64)
-            codes = stage.tile([P, n], U32, name="hid_c", align_bytes=64)
-            scales = stage.tile([P, n], U8, name="hid_s", align_bytes=64)
-            (nc.scalar.copy if c == 0 else nc.vector.tensor_copy)(
-                woven[:].rearrange("p (c i) t -> p c t i", i=4), hid[c][:].rearrange("p t (c i) -> p c t i", i=4)
-            )
+            size, final = CHUNKS[c], c == len(CHUNKS) - 1
+            woven = stage.tile([P, size, PACK], BF16, name="woven", align_bytes=64)
+            codes = stage.tile([P, size], U32, name="hid_c", align_bytes=64)
+            scales = stage.tile([P, size], U8, name="hid_s", align_bytes=64)
+            weave(nc.vector.tensor_copy if final else nc.scalar.copy, woven, hid[c])
             nc.vector.quantize_mx(codes[:].bitcast(FP8X4), scales[:], woven[:].rearrange("p n t -> p (n t)"))
             for a in range(N // P):
-                acc = psum.tile([P, n], F32, name="acc_out")
+                rows = slice(a * P, (a + 1) * P)
+                acc_out = psum.tile([P, size], F32, name="acc_out")
                 nc.tensor.matmul_mx(
-                    acc[:], lhsT=w3_q[0][:, a * P : (a + 1) * P].bitcast(FP8X4), lhsT_scale=w3_q[1][:, a * P : (a + 1) * P],
+                    acc_out[:], lhsT=w3_codes[:, rows].bitcast(FP8X4), lhsT_scale=w3_scales[:, rows],
                     rhs=codes[:].bitcast(FP8X4), rhs_scale=scales[:], start=True, stop=True,
                 )
-                res = work.tile([P, n], F32, name="res")
-                nc.scalar.copy(res[:], acc[:])
-                nc.sync.dma_start(out[a * P : (a + 1) * P, starts[c] : starts[c] + n], res[:])
+                res = work.tile([P, size], F32, name="res")
+                (nc.vector.tensor_copy if final and a == N // P - 1 else nc.scalar.copy)(res[:], acc_out[:])
+                nc.sync.dma_start(out[rows, starts[c] : starts[c] + size], res[:])
 
-        def step(fn, n):
-            if 0 <= n < len(units):
-                fn(n)
-
-        p_window(0)
-        a1(0)
-        p_window(1)
-        for n in range(-2, len(units) + 1):
-            if 0 <= n + 2 < PACK:
-                s_window(n + 2)
-            if 2 <= n + 4 < PACK:
-                p_window(n + 4)
-            step(a1, n + 3)
-            step(b3, n)
-            step(b5, n - 1)
-            step(b1, n + 2)
-            step(a4, n + 2)
-            step(a2, n + 2)
-            step(b4, n)
-            step(b6, n - 1)
-            step(a3, n + 2)
-            step(b2, n + 1)
-            step(a5, n + 2)
-            step(b7, n - 1)
-            if n == 1:
-                prepare_w3()
-            if n >= 1 and units[n - 1][1] == PACK - 1:
-                finish(units[n - 1][0])
+        stages = (
+            (fetch_tp_up, 3), (over_pu2, 0), (gradient, -1), (fetch_sq_up, 2), (tp_difference, 2),
+            (normal_reflection, 2), (shear_term, 0), (times_sin2, -1), (inverse_square, 2),
+            (sq_difference, 1), (share_square, 2), (hidden, -1),
+        )
+        for n in range(-3, len(pieces) + 1):
+            for fn, ahead in stages:
+                if 0 <= n + ahead < len(pieces):
+                    fn(n + ahead)
+            if n >= 1 and pieces[n - 1][0] == PACK - 1:
+                finish(starts.index(pieces[n - 1][1]))

from contextlib import ExitStack

import concourse.mybir as mybir

K, T, S, N, H, U = 512, 1024, 512, 256, 512, 1024
FLOPS = 2 * K * H * S * 2 + 2 * H * N * U

F32 = mybir.dt.float32
BF16 = mybir.dt.bfloat16
I32 = mybir.dt.int32
U32 = mybir.dt.uint32
U16 = mybir.dt.uint16
U8 = mybir.dt.uint8
FP8X4 = mybir.dt.float8_e4m3fn_x4
ACT = mybir.ActivationFunctionType
ALU = mybir.AluOpType

P = 128
PACK = 4
GROUP = 16
WINDOW = S + GROUP

CHUNKS = (512, 256, 256)
PIECES = ((0, 256), (0, 256), (0, 512), (1, 512), (1, 512)) + tuple((j, n) for n in CHUNKS for j in (2, 3))
HEAD, TAIL = 2, 4
FETCH_BUFS = 3
WORK_BUFS = 5


def tile_picked_yshuey_amp_p_kernel(
    tc, x_words, x_scales, w1, w2, sin2, unit, w3, offs, up, dn, out
):
    nc = tc.nc
    with ExitStack() as ctx:
        keep = ctx.enter_context(tc.tile_pool(name="keep", bufs=1))
        work = ctx.enter_context(tc.tile_pool(name="work", bufs=WORK_BUFS))
        stage = ctx.enter_context(tc.tile_pool(name="stage", bufs=len(CHUNKS)))
        psum = ctx.enter_context(tc.psum_pool(name="psum", bufs=4))

        offs_t = keep.tile([P, S // GROUP], U16, name="offs_t")
        up_t = keep.tile([P, U // GROUP], U16, name="up_t")
        dn_t = keep.tile([P, U // GROUP], U16, name="dn_t")
        xw = keep.tile([P, T], U32, name="xw")
        xs = keep.tile([P, T], U8, name="xs")
        unit_t = keep.tile([P, PACK], F32, name="unit_t")
        half = H // 2
        w1_raw = [keep.tile([P, PACK, half], F32, name=f"w1_raw{a}") for a in range(2)]
        w2_raw = [keep.tile([P, PACK, half], F32, name=f"w2_raw{a}") for a in range(2)]
        w3_raw = keep.tile([P, PACK, N], F32, name="w3_raw")
        starts = [sum(CHUNKS[:c]) for c in range(len(CHUNKS))]
        sin_t = [keep.tile([P, U], F32, name=f"sin{j}") for j in range(PACK)]
        tp_table = [keep.tile([P, WINDOW], F32, name=f"tp_table{j}") for j in range(PACK)]
        sq_table = [keep.tile([P, WINDOW], F32, name=f"sq_table{j}") for j in range(PACK)]

        nc.vector.memset(xs[:].bitcast(I32), 0)
        for table in tp_table + sq_table:
            nc.gpsimd.memset(table[:, S:], 0.0)

        nc.sync.dma_start(offs_t[:], offs)
        nc.sync.dma_start(xw[:].bitcast(I32), x_words[0].rearrange("p n t -> p (n t)").bitcast(I32))
        for q in range(4):
            nc.sync.dma_start(xs[32 * q : 32 * q + 4, :].bitcast(I32), x_scales[0, 4 * q : 4 * q + 4, :].bitcast(I32))
        w1_v = w1.rearrange("(p j) c -> p j c", j=PACK)
        w2_v = w2.rearrange("(p j) c -> p j c", j=PACK)
        sin_v = sin2.rearrange("(p j) r -> p j r", j=PACK)
        for a in range(2):
            nc.sync.dma_start(w1_raw[a][:], w1_v[:, :, a * half : (a + 1) * half])
        nc.sync.dma_start(up_t[:], up)
        nc.sync.dma_start(dn_t[:], dn)
        for a in range(2):
            nc.sync.dma_start(w2_raw[a][:], w2_v[:, :, a * half : (a + 1) * half])
        nc.sync.dma_start(unit_t[:], unit.rearrange("(p j) o -> p (j o)", j=PACK))
        nc.sync.dma_start(w3_raw[:], w3.rearrange("(p j) c -> p j c", j=PACK))
        for j in range(PACK):
            nc.sync.dma_start(sin_t[j][:], sin_v[:, j, :])

        xg = keep.tile([P, S], U32, name="xg", align_bytes=64)
        xsg = keep.tile([P, S], U8, name="xsg", align_bytes=64)
        nc.vector.tensor_copy(xg[:], xw[:].indirect(offs_t[:]))
        nc.vector.tensor_copy(xsg[:], xs[:].indirect(offs_t[:]))

        def dealt_weights(raw, name, copies):
            grouped = keep.tile([P, PACK * H], BF16, name=name + "_g", align_bytes=64)
            codes = keep.tile([P, H], U32, name=name + "_c", align_bytes=64)
            scales = keep.tile([P, H], U8, name=name + "_s", align_bytes=64)
            view = grouped[:].rearrange("p (t m j) -> p m t j", t=PACK, j=PACK)
            m_half = half // PACK
            for a in range(2):
                copies[a](view[:, a * m_half : (a + 1) * m_half], raw[a][:].rearrange("p j (m t) -> p m t j", t=PACK))
            for lo, hi in ((0, P), (P, H)):
                nc.vector.quantize_mx(codes[:, lo:hi].bitcast(FP8X4), scales[:, lo:hi], grouped[:, PACK * lo : PACK * hi])
            return codes, scales

        def product(weights, j):
            codes, scales = weights
            acc = psum.tile([P, S], F32, name="acc")
            nc.tensor.matmul_mx(
                acc[:], lhsT=codes[:, j * P : (j + 1) * P].bitcast(FP8X4), lhsT_scale=scales[:, j * P : (j + 1) * P],
                rhs=xg[:].bitcast(FP8X4), rhs_scale=xsg[:], start=True, stop=True,
            )
            return acc

        w1_q = dealt_weights(w1_raw, "w1", (nc.scalar.copy, nc.vector.tensor_copy))
        w2_q = dealt_weights(w2_raw, "w2", (nc.vector.tensor_copy, nc.vector.tensor_copy))
        neg_half_unit = keep.tile([P, PACK], F32, name="neg_half_unit")
        nc.vector.tensor_scalar(neg_half_unit[:], unit_t[:], -0.5, None, ALU.mult)

        pieces = [(j, sum(w for i, w in PIECES[:k] if i == j), width) for k, (j, width) in enumerate(PIECES)]
        held = [{} for piece in pieces]
        hid = [keep.tile([P, PACK, size], BF16, name=f"hid{c}") for c, size in enumerate(CHUNKS)]

        def new(n, key, bufs=WORK_BUFS):
            held[n][key] = work.tile([P, pieces[n][2]], F32, name=key, bufs=bufs)
            return held[n][key][:]

        def looked_up(tables, lst, n):
            j, lo, width = pieces[n]
            return tables[j][:].indirect(lst[:, lo // GROUP : (lo + width) // GROUP])

        def fetch_up(tables, n, key):
            if n < HEAD:
                nc.vector.tensor_copy(new(n, key, FETCH_BUFS), looked_up(tables, up_t, n))
            else:
                nc.scalar.activation(new(n, key, FETCH_BUFS), looked_up(tables, up_t, n), ACT.Copy, scale=-1.0)

        def minus_up(n):
            return ALU.subtract if n < HEAD else ALU.add

        def fetch_tp_up(n):
            j, lo, width = pieces[n]
            if lo == 0:
                nc.scalar.activation(tp_table[j][:, :S], product(w1_q, j)[:], ACT.Tanh)
            fetch_up(tp_table, n, "tp_up")

        def fetch_sq_up(n):
            j, lo, width = pieces[n]
            if lo == 0:
                tan_s = stage.tile([P, S], F32, name="tan_s")
                nc.scalar.activation(tan_s[:], product(w2_q, j)[:], ACT.Tanh)
                nc.scalar.activation(sq_table[j][:, :S], tan_s[:], ACT.Exp)
            fetch_up(sq_table, n, "sq_up")
            if n >= len(pieces) - TAIL:
                nc.scalar.activation(new(n, "sq_dn", FETCH_BUFS), looked_up(sq_table, dn_t, n), ACT.Copy)

        def inverse_square(n):
            nc.scalar.activation(new(n, "inv_pu2"), held[n]["tp_up"][:], ACT.Exp, scale=-1.0 if n < HEAD else 1.0)

        def normal_reflection(n):
            nc.scalar.activation(new(n, "r0"), held[n]["tp_diff"][:], ACT.Tanh, scale=0.25)

        def share_square(n):
            nc.scalar.activation(new(n, "share2"), held[n]["r0"][:], ACT.Square, bias=-1.0)

        def tp_difference(n):
            nc.vector.tensor_tensor(new(n, "tp_diff"), looked_up(tp_table, dn_t, n), held[n]["tp_up"][:], minus_up(n))

        def sq_difference(n):
            lower = held[n]["sq_dn"][:] if "sq_dn" in held[n] else looked_up(sq_table, dn_t, n)
            nc.vector.tensor_tensor(new(n, "chain"), lower, held[n]["sq_up"][:], minus_up(n))

        def over_pu2(n):
            chain = held[n]["chain"][:]
            nc.vector.tensor_tensor(chain, chain, held[n]["inv_pu2"][:], ALU.mult)

        def shear_term(n):
            j, chain = pieces[n][0], held[n]["chain"][:]
            nc.vector.scalar_tensor_tensor(chain, chain, neg_half_unit[:, j : j + 1], held[n]["share2"][:], ALU.mult, ALU.mult)

        def gradient(n):
            j, chain = pieces[n][0], held[n]["chain"][:]
            nc.vector.scalar_tensor_tensor(chain, held[n]["r0"][:], unit_t[:, j : j + 1], chain, ALU.mult, ALU.add)

        def times_sin2(n):
            j, lo, width = pieces[n]
            chain = held[n]["chain"][:]
            nc.vector.tensor_tensor(chain, chain, sin_t[j][:, lo : lo + width], ALU.mult)

        def hidden(n):
            j, lo, width = pieces[n]
            for c, size in enumerate(CHUNKS):
                first, last = max(lo, starts[c]), min(lo + width, starts[c] + size)
                if first < last:
                    nc.vector.scalar_tensor_tensor(
                        hid[c][:, j, first - starts[c] : last - starts[c]], held[n]["r0"][:, first - lo : last - lo],
                        unit_t[:, j : j + 1], held[n]["chain"][:, first - lo : last - lo], ALU.mult, ALU.add,
                    )

        def weave(copy, woven, rows):
            copy(woven[:].rearrange("p (c i) j -> p c j i", i=4), rows[:].rearrange("p j (c i) -> p c j i", i=4))

        w3_woven = keep.tile([P, N, PACK], BF16, name="w3_g", align_bytes=64)
        w3_codes = keep.tile([P, N], U32, name="w3_c", align_bytes=64)
        w3_scales = keep.tile([P, N], U8, name="w3_s", align_bytes=64)
        weave(nc.vector.tensor_copy, w3_woven, w3_raw)
        nc.vector.quantize_mx(w3_codes[:].bitcast(FP8X4), w3_scales[:], w3_woven[:].rearrange("p n t -> p (n t)"))

        def finish(c):
            size, final = CHUNKS[c], c == len(CHUNKS) - 1
            woven = stage.tile([P, size, PACK], BF16, name="woven", align_bytes=64)
            codes = stage.tile([P, size], U32, name="hid_c", align_bytes=64)
            scales = stage.tile([P, size], U8, name="hid_s", align_bytes=64)
            weave(nc.vector.tensor_copy if final else nc.scalar.copy, woven, hid[c])
            nc.vector.quantize_mx(codes[:].bitcast(FP8X4), scales[:], woven[:].rearrange("p n t -> p (n t)"))
            for a in range(N // P):
                rows = slice(a * P, (a + 1) * P)
                acc_out = psum.tile([P, size], F32, name="acc_out")
                nc.tensor.matmul_mx(
                    acc_out[:], lhsT=w3_codes[:, rows].bitcast(FP8X4), lhsT_scale=w3_scales[:, rows],
                    rhs=codes[:].bitcast(FP8X4), rhs_scale=scales[:], start=True, stop=True,
                )
                res = work.tile([P, size], F32, name="res")
                (nc.vector.tensor_copy if final and a == N // P - 1 else nc.scalar.copy)(res[:], acc_out[:])
                nc.sync.dma_start(out[rows, starts[c] : starts[c] + size], res[:])

        stages = (
            (fetch_tp_up, 3), (over_pu2, 0), (gradient, -1), (fetch_sq_up, 2), (tp_difference, 2),
            (normal_reflection, 2), (shear_term, 0), (times_sin2, -1), (inverse_square, 2),
            (sq_difference, 1), (share_square, 2), (hidden, -1),
        )
        for n in range(-3, len(pieces) + 1):
            for fn, ahead in stages:
                if 0 <= n + ahead < len(pieces):
                    fn(n + ahead)
            if n >= 1 and pieces[n - 1][0] == PACK - 1:
                finish(starts.index(pieces[n - 1][1]))
